import numpy as np
import ml_dtypes


def mxq(x, axis, fmt="e4m3"):
    dtype, down = {"e4m3": (ml_dtypes.float8_e4m3fn, 7), "e5m2": (ml_dtypes.float8_e5m2, 14)}[fmt]
    v = np.moveaxis(np.asarray(x, np.float32).astype(ml_dtypes.bfloat16).astype(np.float64), axis, -1)
    blocks = v.reshape(v.shape[:-1] + (-1, 32))
    amax = np.abs(blocks).max(-1, keepdims=True)
    byte = np.maximum(np.where(amax > 0, np.frexp(amax)[1] - 1 + 127, 0) - down, 1)
    scale = np.exp2(byte - 127.0)
    codes = (blocks / scale).astype(np.float32).astype(dtype).astype(np.float64)
    return np.moveaxis((codes * scale).reshape(v.shape), -1, axis)


WIDE = False


def mx_kscale(k):
    if not WIDE:
        return np.ones(k)
    levels = np.array([10, -10, 5, -5, 0])
    if k % 512:
        return np.exp2(np.random.permutation(np.resize(levels, k // 32))).repeat(32)
    a = np.empty((k // 512, 16))
    for p in range(k // 512):
        a[p, :8] = np.random.permutation(np.resize(levels, 8))
        for g in range(8):
            far = levels[np.abs(levels - a[p, g]) >= 10]
            a[p, g + 8] = far[np.random.randint(len(far))]
    return np.exp2(a.ravel()).repeat(32)


def f64(x):
    return np.asarray(x).astype(np.float64)


def striped(idx):
    return np.tile(np.asarray(idx).reshape(-1, 16).T, (8, 1)).astype(np.uint16)


def unstriped(offs):
    return offs[:16].T.reshape(-1).astype(np.int64)


E2M1 = np.array([0.0, 0.5, 1.0, 1.5, 2.0, 3.0, 4.0, 6.0, -0.0, -0.5, -1.0, -1.5, -2.0, -3.0, -4.0, -6.0])


def pack_weight(w, fmt):
    k, n = w.shape
    w = f64(np.asarray(w, np.float32).astype(ml_dtypes.bfloat16)).reshape(k // 32, 32, n)
    amax = np.abs(w).max(1)
    if fmt == "e4m3":
        byte = np.frexp(amax)[1] - 1 + 127 - 7
    else:
        mant, ex = np.frexp(amax / 6.0)
        byte = np.where(mant > 0.5, ex, ex - 1) + 127
    byte = np.clip(np.where(amax > 0, byte, 1), 1, 254)
    scaled = (w * np.exp2(127.0 - byte)[:, None, :]).reshape(k, n).astype(np.float32)
    by_word = np.ascontiguousarray(scaled.reshape(k // 512, 128, 4, n).transpose(0, 1, 3, 2))
    if fmt == "e4m3":
        words = by_word.astype(ml_dtypes.float8_e4m3fn).view(np.uint8)
    else:
        c = by_word.astype(ml_dtypes.float4_e2m1fn).view(np.uint8) & 0xF
        words = (c[..., 0::2] | (c[..., 1::2] << 4)).reshape(k // 512, 128, 2 * n)
    return np.ascontiguousarray(words), np.ascontiguousarray(byte.astype(np.uint8).reshape(k // 512, 16, n))


def unpack_weight(words, scales, fmt):
    g, _, n = scales.shape
    words = np.ascontiguousarray(words).reshape(g, 128, n, -1)
    if fmt == "e4m3":
        vals = words.view(ml_dtypes.float8_e4m3fn).astype(np.float64)
    else:
        nib = np.empty((g, 128, n, 4), np.uint8)
        nib[..., 0::2] = words & 0xF
        nib[..., 1::2] = words >> 4
        vals = E2M1[nib]
    vals = vals * np.repeat(np.exp2(scales.astype(np.float64) - 127.0), 8, axis=1)[..., None]
    return vals.transpose(0, 1, 3, 2).reshape(g * 512, n)


K, T, C, J, B, L = 1024, 256, 2048, 512, 64, 512


def setup_inputs():
    n = np.random.standard_normal
    idx = np.random.permutation(C)[:J]
    fk = mx_kscale(K)
    fl = mx_kscale(L)
    xtp = pack_weight(n((K, T)) * np.random.uniform(0.1, 1.2, (1, T)) / fk[:, None], "e2m1")
    wcp = pack_weight(n((K, C)) * 1 / np.sqrt(K) * fk[:, None], "e4m3")
    wsp = pack_weight(n((L, B)) * 1 / np.sqrt(L) * fl[:, None], "e2m1")
    return {
        "xt_words": xtp[0],
        "xt_scales": xtp[1],
        "wc_words": wcp[0],
        "wc_scales": wcp[1],
        "xs": (n((L, T)) / fl[:, None]).astype(np.float32),
        "ws_words": wsp[0],
        "ws_scales": wsp[1],
        "offs": striped(idx),
    }


def reference(xt_words, xt_scales, wc_words, wc_scales, xs, ws_words, ws_scales, offs):
    idx = unstriped(offs)
    xtu = unpack_weight(xt_words, xt_scales, "e2m1")
    wcu = unpack_weight(wc_words, wc_scales, "e4m3")
    wsu = unpack_weight(ws_words, ws_scales, "e2m1")
    wcidxg = wcu[:, idx]
    z = xtu.T @ wcidxg
    p = np.exp(z)
    fs = p.reshape(T, B, J // B).sum(axis=2)
    xsq = mxq(f64(xs), 0, "e4m3")
    s = xsq.T @ wsu
    y = np.log(fs) - np.log(np.sum(p, axis=1, keepdims=True)) + 0.5 * s
    return y

@@ -1,0 +1,187 @@
+from contextlib import ExitStack
+
+import concourse.mybir as mybir
+
+K, T, C, J, B, L = 1024, 256, 2048, 512, 64, 512
+FLOPS = 2 * T * K * J + 2 * T * L * B
+
+F32 = mybir.dt.float32
+BF16 = mybir.dt.bfloat16
+I32 = mybir.dt.int32
+U32 = mybir.dt.uint32
+U16 = mybir.dt.uint16
+U8 = mybir.dt.uint8
+FP8X4 = mybir.dt.float8_e4m3fn_x4
+FP4X4 = mybir.dt.float4_e2m1fn_x4
+ALU = mybir.AluOpType
+ACT = mybir.ActivationFunctionType
+AXIS = mybir.AxisListType
+
+P = 128
+PACK = 4
+PASSES = K // (P * PACK)
+TILES = T // P
+SLOTS = J // B
+HALVES = 2
+JH = J // HALVES
+BH = B // HALVES
+ROWS_AT = P - 16 * PASSES
+
+
+def load_scale_rows(queue, plane, scales):
+    rows = scales.rearrange("z (q r) c -> r q z c", r=4)
+    for r in range(4):
+        queue.dma_start(out=plane[r:P:32, :, :].bitcast(I32), in_=rows[r].bitcast(I32))
+
+
+def tile_list_class_families_kernel(tc, xt_words, xt_scales, wc_words, wc_scales, xs, ws_words, ws_scales, offs, out):
+    nc = tc.nc
+    with ExitStack() as ctx:
+        keep = ctx.enter_context(tc.tile_pool(name="keep", bufs=1))
+        psum = ctx.enter_context(tc.psum_pool(name="psum", bufs=1))
+
+        offsets = keep.tile([P, J // 16], U16, name="offsets")
+        nc.sync.dma_start(offsets[:], offs)
+
+        wc_rows = keep.tile([P, C], U8, name="wc_rows", align_bytes=64)
+        picked_plane = keep.tile([P, PASSES, J], U8, name="picked_plane", align_bytes=64)
+        xt_plane = keep.tile([P, PASSES, T], U8, name="xt_plane", align_bytes=64)
+        ws_plane = keep.tile([P, 1, B], U8, name="ws_plane", align_bytes=64)
+        nc.scalar.dma_start(
+            out=wc_rows[ROWS_AT:P, :].bitcast(I32), in_=wc_scales.rearrange("z g c -> g z c").bitcast(I32)
+        )
+        nc.vector.memset(wc_rows[0:ROWS_AT, :].bitcast(I32), 0)
+        nc.vector.memset(picked_plane[:].bitcast(I32), 0)
+        nc.gpsimd.memset(xt_plane[:].bitcast(I32), 0)
+        nc.gpsimd.memset(ws_plane[:].bitcast(I32), 0)
+
+        table = [keep.tile([P, C], I32, name=f"table{z}", align_bytes=64) for z in range(PASSES)]
+        xt_codes = keep.tile([P, PASSES, 2 * T], U8, name="xt_codes", align_bytes=64)
+        xs_raw = keep.tile([P, PACK, T], F32, name="xs_raw", align_bytes=64)
+        ws_codes = keep.tile([P, 2 * B], U8, name="ws_codes", align_bytes=64)
+
+        nc.sync.dma_start(out=table[0][:], in_=wc_words[0].rearrange("p c r -> p (c r)").bitcast(I32))
+        nc.sync.dma_start(out=xt_codes[:].bitcast(I32), in_=xt_words.rearrange("z p b -> p z b").bitcast(I32))
+        nc.sync.dma_start(out=table[1][:], in_=wc_words[1].rearrange("p c r -> p (c r)").bitcast(I32))
+        nc.sync.dma_start(out=xs_raw[:], in_=xs.rearrange("(p j) t -> p j t", j=PACK))
+        load_scale_rows(nc.gpsimd, xt_plane, xt_scales)
+        nc.gpsimd.dma_start(out=ws_codes[:].bitcast(I32), in_=ws_words[0].bitcast(I32))
+        load_scale_rows(nc.gpsimd, ws_plane, ws_scales)
+
+        picked_rows = keep.tile([P, J], U8, name="picked_rows", align_bytes=64)
+        nc.vector.tensor_copy(picked_rows[:], wc_rows[:].indirect(offsets[:]))
+        for q in range(4):
+            nc.scalar.dma_start(
+                out=picked_plane[32 * q : 32 * q + 4, :, :].bitcast(I32),
+                in_=picked_rows[ROWS_AT + 8 * q : ROWS_AT + 8 * q + 8, :].bitcast(I32),
+            )
+
+        picked = [[keep.tile([P, JH], U32, name=f"picked{z}{a}", align_bytes=64) for a in range(HALVES)] for z in range(PASSES)]
+        logits = [[psum.tile([P, JH], F32, name=f"logits{a}{h}") for h in range(TILES)] for a in range(HALVES)]
+        for z in range(PASSES):
+            for a in range(HALVES):
+                cols = slice(a * JH // 16, (a + 1) * JH // 16)
+                nc.vector.tensor_copy(picked[z][a][:], table[z][:].bitcast(U32).indirect(offsets[:, cols]))
+                for h in range(TILES):
+                    nc.tensor.matmul_mx(
+                        out=logits[a][h][:],
+                        lhsT=xt_codes[:, z, 2 * P * h : 2 * P * (h + 1)].bitcast(FP4X4),
+                        lhsT_scale=xt_plane[:, z, P * h : P * (h + 1)],
+                        rhs=picked[z][a][:].bitcast(FP8X4),
+                        rhs_scale=picked_plane[:, z, a * JH : (a + 1) * JH],
+                        start=(z == 0),
+                        stop=(z == PASSES - 1),
+                    )
+
+        xs_grouped = keep.tile([P, T, PACK], BF16, name="xs_grouped", align_bytes=64)
+        nc.scalar.copy(out=xs_grouped[:], in_=xs_raw[:].rearrange("p j t -> p t j"))
+
+        fam_max = keep.tile([P, TILES, B], F32, name="fam_max")
+        shifted = keep.tile([P, HALVES, TILES, JH], F32, name="shifted")
+        expd = keep.tile([P, HALVES, TILES, JH], F32, name="expd")
+        for a in range(HALVES):
+            for h in range(TILES):
+                nc.vector.tensor_reduce(
+                    out=fam_max[:, h, a * BH : (a + 1) * BH],
+                    in_=logits[a][h][:].rearrange("p (b s) -> p b s", s=SLOTS),
+                    axis=AXIS.X,
+                    op=ALU.max,
+                )
+        row_max = keep.tile([P, TILES], F32, name="row_max")
+        nc.vector.tensor_reduce(out=row_max[:], in_=fam_max[:], axis=AXIS.X, op=ALU.max)
+        below = keep.tile([P, TILES, B], F32, name="below")
+        weight = keep.tile([P, TILES, B], F32, name="weight")
+        for a in range(HALVES):
+            for h in range(TILES):
+                nc.vector.tensor_tensor(
+                    out=shifted[:, a, h, :].rearrange("p (b s) -> p b s", s=SLOTS),
+                    in0=logits[a][h][:].rearrange("p (b s) -> p b s", s=SLOTS),
+                    in1=fam_max[:, h, a * BH : (a + 1) * BH].unsqueeze(2).to_broadcast([P, BH, SLOTS]),
+                    op=ALU.subtract,
+                )
+                nc.scalar.activation(out=expd[:, a, h, :], in_=shifted[:, a, h, :], func=ACT.Exp)
+                if a == 0 and h == 0:
+                    nc.vector.tensor_tensor(
+                        out=below[:],
+                        in0=fam_max[:],
+                        in1=row_max[:].unsqueeze(2).to_broadcast([P, TILES, B]),
+                        op=ALU.subtract,
+                    )
+                    nc.scalar.activation(out=weight[:], in_=below[:], func=ACT.Exp)
+
+        xs_codes = keep.tile([P, T], U32, name="xs_codes", align_bytes=64)
+        xs_plane = keep.tile([P, T], U8, name="xs_plane", align_bytes=64)
+        nc.vector.quantize_mx(
+            out=xs_codes[:].bitcast(FP8X4), scales=xs_plane[:], in_=xs_grouped[:].rearrange("p t j -> p (t j)")
+        )
+        base = keep.tile([P, TILES, B], F32, name="base")
+        fam = [psum.tile([P, B], F32, name=f"fam{h}") for h in range(TILES)]
+        for h in range(TILES):
+            nc.tensor.matmul_mx(
+                out=fam[h][:],
+                lhsT=xs_codes[:, P * h : P * (h + 1)].bitcast(FP8X4),
+                lhsT_scale=xs_plane[:, P * h : P * (h + 1)],
+                rhs=ws_codes[:].bitcast(FP4X4),
+                rhs_scale=ws_plane[:, 0, :],
+                start=True,
+                stop=True,
+            )
+
+        sums = keep.tile([P, TILES, B + 1], F32, name="sums")
+        for a in range(HALVES):
+            nc.vector.tensor_reduce(
+                out=sums[:, :, a * BH : (a + 1) * BH],
+                in_=expd[:, a, :, :].rearrange("p h (b s) -> p h b s", s=SLOTS),
+                axis=AXIS.X,
+                op=ALU.add,
+            )
+
+        weighted = keep.tile([P, TILES, B], F32, name="weighted")
+        for h in range(TILES):
+            nc.vector.scalar_tensor_tensor(
+                out=weighted[:, h, :],
+                in0=sums[:, h, 0:B],
+                scalar=1.0,
+                in1=weight[:, h, :],
+                op0=ALU.mult,
+                op1=ALU.mult,
+                accum_out=sums[:, h, B : B + 1],
+            )
+        for h in range(TILES):
+            nc.vector.scalar_tensor_tensor(
+                out=base[:, h, :], in0=fam[h][:], scalar=0.5, in1=below[:, h, :], op0=ALU.mult, op1=ALU.add
+            )
+
+        logs = keep.tile([P, TILES, B + 1], F32, name="logs")
+        nc.scalar.activation(out=logs[:], in_=sums[:], func=ACT.Ln)
+        result = keep.tile([P, TILES, B], F32, name="result")
+        for h in range(TILES):
+            nc.vector.scalar_tensor_tensor(
+                out=result[:, h, :],
+                in0=logs[:, h, 0:B],
+                scalar=logs[:, h, B : B + 1],
+                in1=base[:, h, :],
+                op0=ALU.subtract,
+                op1=ALU.add,
+            )
+        nc.sync.dma_start(out=out.rearrange("(h p) b -> p h b", p=P), in_=result[:])

@@ -64,7 +64,7 @@ def tile_list_class_families_kernel(tc, xt_words, xt_scales, wc_words, wc_scales
         nc.sync.dma_start(out=xt_codes[:].bitcast(I32), in_=xt_words.rearrange("z p b -> p z b").bitcast(I32))
         nc.sync.dma_start(out=table[1][:], in_=wc_words[1].rearrange("p c r -> p (c r)").bitcast(I32))
         nc.sync.dma_start(out=xs_raw[:], in_=xs.rearrange("(p j) t -> p j t", j=PACK))
-        load_scale_rows(nc.gpsimd, xt_plane, xt_scales)
+        load_scale_rows(nc.scalar, xt_plane, xt_scales)
         nc.gpsimd.dma_start(out=ws_codes[:].bitcast(I32), in_=ws_words[0].bitcast(I32))
         load_scale_rows(nc.gpsimd, ws_plane, ws_scales)
 
@@ -77,20 +77,20 @@ def tile_list_class_families_kernel(tc, xt_words, xt_scales, wc_words, wc_scales
             )
 
         picked = [[keep.tile([P, JH], U32, name=f"picked{z}{a}", align_bytes=64) for a in range(HALVES)] for z in range(PASSES)]
-        logits = [[psum.tile([P, JH], F32, name=f"logits{a}{h}") for h in range(TILES)] for a in range(HALVES)]
+        logits = [psum.tile([P, TILES, JH], F32, name=f"logits{a}") for a in range(HALVES)]
         for z in range(PASSES):
             for a in range(HALVES):
                 cols = slice(a * JH // 16, (a + 1) * JH // 16)
                 nc.vector.tensor_copy(picked[z][a][:], table[z][:].bitcast(U32).indirect(offsets[:, cols]))
                 for h in range(TILES):
                     nc.tensor.matmul_mx(
-                        out=logits[a][h][:],
+                        out=logits[a][:, h, :],
                         lhsT=xt_codes[:, z, 2 * P * h : 2 * P * (h + 1)].bitcast(FP4X4),
                         lhsT_scale=xt_plane[:, z, P * h : P * (h + 1)],
                         rhs=picked[z][a][:].bitcast(FP8X4),
                         rhs_scale=picked_plane[:, z, a * JH : (a + 1) * JH],
-                        start=(z == 0),
-                        stop=(z == PASSES - 1),
+                        start=(z == 0 and h == 0),
+                        stop=(z == PASSES - 1 and h == TILES - 1),
                     )
 
         xs_grouped = keep.tile([P, T, PACK], BF16, name="xs_grouped", align_bytes=64)
@@ -100,35 +100,31 @@ def tile_list_class_families_kernel(tc, xt_words, xt_scales, wc_words, wc_scales
         shifted = keep.tile([P, HALVES, TILES, JH], F32, name="shifted")
         expd = keep.tile([P, HALVES, TILES, JH], F32, name="expd")
         for a in range(HALVES):
-            for h in range(TILES):
-                nc.vector.tensor_reduce(
-                    out=fam_max[:, h, a * BH : (a + 1) * BH],
-                    in_=logits[a][h][:].rearrange("p (b s) -> p b s", s=SLOTS),
-                    axis=AXIS.X,
-                    op=ALU.max,
-                )
-        row_max = keep.tile([P, TILES], F32, name="row_max")
-        nc.vector.tensor_reduce(out=row_max[:], in_=fam_max[:], axis=AXIS.X, op=ALU.max)
-        below = keep.tile([P, TILES, B], F32, name="below")
+            nc.vector.tensor_reduce(
+                out=fam_max[:, :, a * BH : (a + 1) * BH],
+                in_=logits[a][:].rearrange("p h (b s) -> p h b s", s=SLOTS),
+                axis=AXIS.X,
+                op=ALU.max,
+            )
+        neg_row_max = keep.tile([P, TILES], F32, name="neg_row_max")
+        nc.vector.tensor_reduce(out=neg_row_max[:], in_=fam_max[:], axis=AXIS.X, op=ALU.max, negate=True)
         weight = keep.tile([P, TILES, B], F32, name="weight")
-        for a in range(HALVES):
-            for h in range(TILES):
-                nc.vector.tensor_tensor(
-                    out=shifted[:, a, h, :].rearrange("p (b s) -> p b s", s=SLOTS),
-                    in0=logits[a][h][:].rearrange("p (b s) -> p b s", s=SLOTS),
-                    in1=fam_max[:, h, a * BH : (a + 1) * BH].unsqueeze(2).to_broadcast([P, BH, SLOTS]),
-                    op=ALU.subtract,
-                )
-                nc.scalar.activation(out=expd[:, a, h, :], in_=shifted[:, a, h, :], func=ACT.Exp)
-                if a == 0 and h == 0:
-                    nc.vector.tensor_tensor(
-                        out=below[:],
-                        in0=fam_max[:],
-                        in1=row_max[:].unsqueeze(2).to_broadcast([P, TILES, B]),
-                        op=ALU.subtract,
-                    )
-                    nc.scalar.activation(out=weight[:], in_=below[:], func=ACT.Exp)
+        for h in range(TILES):
+            nc.scalar.activation(out=weight[:, h, :], in_=fam_max[:, h, :], func=ACT.Exp, bias=neg_row_max[:, h : h + 1])
+        for a, tiles in ((0, slice(0, 2)), (1, slice(0, 1)), (1, slice(1, 2))):
+            n = tiles.stop - tiles.start
+            nc.vector.tensor_tensor(
+                out=shifted[:, a, tiles, :].rearrange("p h (b s) -> p h b s", s=SLOTS),
+                in0=logits[a][:, tiles, :].rearrange("p h (b s) -> p h b s", s=SLOTS),
+                in1=fam_max[:, tiles, a * BH : (a + 1) * BH].unsqueeze(3).to_broadcast([P, n, BH, SLOTS]),
+                op=ALU.subtract,
+            )
+            nc.scalar.activation(out=expd[:, a, tiles, :], in_=shifted[:, a, tiles, :], func=ACT.Exp)
 
+        below = keep.tile([P, TILES, B], F32, name="below")
+        nc.vector.tensor_tensor(
+            out=below[:], in0=fam_max[:], in1=neg_row_max[:].unsqueeze(2).to_broadcast([P, TILES, B]), op=ALU.add
+        )
         xs_codes = keep.tile([P, T], U32, name="xs_codes", align_bytes=64)
         xs_plane = keep.tile([P, T], U8, name="xs_plane", align_bytes=64)
         nc.vector.quantize_mx(

@@ -26,12 +26,9 @@ HALVES = 2
 JH = J // HALVES
 BH = B // HALVES
 ROWS_AT = P - 16 * PASSES
-
-
-def load_scale_rows(queue, plane, scales):
-    rows = scales.rearrange("z (q r) c -> r q z c", r=4)
-    for r in range(4):
-        queue.dma_start(out=plane[r:P:32, :, :].bitcast(I32), in_=rows[r].bitcast(I32))
+XT_AT = J
+WS_AT = XT_AT + T
+ROW = WS_AT + B
 
 
 def tile_list_class_families_kernel(tc, xt_words, xt_scales, wc_words, wc_scales, xs, ws_words, ws_scales, offs, out):
@@ -40,57 +37,60 @@ def tile_list_class_families_kernel(tc, xt_words, xt_scales, wc_words, wc_scales
         keep = ctx.enter_context(tc.tile_pool(name="keep", bufs=1))
         psum = ctx.enter_context(tc.psum_pool(name="psum", bufs=1))
 
+        reuse = ctx.enter_context(tc.tile_pool(name="reuse", bufs=1))
         offsets = keep.tile([P, J // 16], U16, name="offsets")
-        nc.sync.dma_start(offsets[:], offs)
-
         wc_rows = keep.tile([P, C], U8, name="wc_rows", align_bytes=64)
-        picked_plane = keep.tile([P, PASSES, J], U8, name="picked_plane", align_bytes=64)
-        xt_plane = keep.tile([P, PASSES, T], U8, name="xt_plane", align_bytes=64)
-        ws_plane = keep.tile([P, 1, B], U8, name="ws_plane", align_bytes=64)
-        nc.scalar.dma_start(
-            out=wc_rows[ROWS_AT:P, :].bitcast(I32), in_=wc_scales.rearrange("z g c -> g z c").bitcast(I32)
-        )
+        stage = keep.tile([P, ROW], U8, name="stage", align_bytes=64)
+        planes = keep.tile([P, PASSES, ROW], U8, name="planes", align_bytes=64)
+        nc.gpsimd.memset(stage[ROWS_AT:P, WS_AT:ROW].bitcast(I32), 0)
         nc.vector.memset(wc_rows[0:ROWS_AT, :].bitcast(I32), 0)
-        nc.vector.memset(picked_plane[:].bitcast(I32), 0)
-        nc.gpsimd.memset(xt_plane[:].bitcast(I32), 0)
-        nc.gpsimd.memset(ws_plane[:].bitcast(I32), 0)
+        nc.gpsimd.memset(planes[:].bitcast(I32), 0)
 
         table = [keep.tile([P, C], I32, name=f"table{z}", align_bytes=64) for z in range(PASSES)]
+        xs_raw = reuse.tile([P, PACK, T], F32, name="xs_raw", align_bytes=64, offset=0)
+        picked_rows = reuse.tile([P, J], U8, name="picked_rows", align_bytes=64, offset=0)
         xt_codes = keep.tile([P, PASSES, 2 * T], U8, name="xt_codes", align_bytes=64)
-        xs_raw = keep.tile([P, PACK, T], F32, name="xs_raw", align_bytes=64)
         ws_codes = keep.tile([P, 2 * B], U8, name="ws_codes", align_bytes=64)
 
+        nc.sync.dma_start(
+            out=wc_rows[ROWS_AT:P, :].bitcast(I32), in_=wc_scales.rearrange("z g c -> g z c").bitcast(I32)
+        )
+        nc.sync.dma_start(offsets[:], offs)
         nc.sync.dma_start(out=table[0][:], in_=wc_words[0].rearrange("p c r -> p (c r)").bitcast(I32))
-        nc.sync.dma_start(out=xt_codes[:].bitcast(I32), in_=xt_words.rearrange("z p b -> p z b").bitcast(I32))
+        nc.sync.dma_start(
+            out=stage[ROWS_AT:P, XT_AT:WS_AT].bitcast(I32), in_=xt_scales.rearrange("z g c -> g z c").bitcast(I32)
+        )
+        nc.sync.dma_start(out=stage[ROWS_AT:P:PASSES, WS_AT:ROW].bitcast(I32), in_=ws_scales[0].bitcast(I32))
         nc.sync.dma_start(out=table[1][:], in_=wc_words[1].rearrange("p c r -> p (c r)").bitcast(I32))
-        nc.sync.dma_start(out=xs_raw[:], in_=xs.rearrange("(p j) t -> p j t", j=PACK))
-        load_scale_rows(nc.scalar, xt_plane, xt_scales)
-        nc.gpsimd.dma_start(out=ws_codes[:].bitcast(I32), in_=ws_words[0].bitcast(I32))
-        load_scale_rows(nc.gpsimd, ws_plane, ws_scales)
+        nc.sync.dma_start(out=xt_codes[:].bitcast(I32), in_=xt_words.rearrange("z p b -> p z b").bitcast(I32))
+        nc.sync.dma_start(out=ws_codes[:].bitcast(I32), in_=ws_words[0].bitcast(I32))
 
-        picked_rows = keep.tile([P, J], U8, name="picked_rows", align_bytes=64)
         nc.vector.tensor_copy(picked_rows[:], wc_rows[:].indirect(offsets[:]))
+        nc.vector.tensor_copy(stage[ROWS_AT:P, 0:J].bitcast(I32), picked_rows[ROWS_AT:P, :].bitcast(I32))
         for q in range(4):
-            nc.scalar.dma_start(
-                out=picked_plane[32 * q : 32 * q + 4, :, :].bitcast(I32),
-                in_=picked_rows[ROWS_AT + 8 * q : ROWS_AT + 8 * q + 8, :].bitcast(I32),
+            nc.sync.dma_start(
+                out=planes[32 * q : 32 * q + 4, :, :].bitcast(I32),
+                in_=stage[ROWS_AT + 8 * q : ROWS_AT + 8 * q + 8, :].bitcast(I32),
             )
+        nc.sync.dma_start(out=xs_raw[:], in_=xs.rearrange("(p j) t -> p j t", j=PACK))
 
         picked = [[keep.tile([P, JH], U32, name=f"picked{z}{a}", align_bytes=64) for a in range(HALVES)] for z in range(PASSES)]
-        logits = [psum.tile([P, TILES, JH], F32, name=f"logits{a}") for a in range(HALVES)]
+        logits = [[psum.tile([P, JH], F32, name=f"logits{a}{h}") for h in range(TILES)] for a in range(HALVES)]
         for z in range(PASSES):
             for a in range(HALVES):
                 cols = slice(a * JH // 16, (a + 1) * JH // 16)
                 nc.vector.tensor_copy(picked[z][a][:], table[z][:].bitcast(U32).indirect(offsets[:, cols]))
-                for h in range(TILES):
+        for a in range(HALVES):
+            for h in range(TILES):
+                for z in range(PASSES):
                     nc.tensor.matmul_mx(
-                        out=logits[a][:, h, :],
+                        out=logits[a][h][:],
                         lhsT=xt_codes[:, z, 2 * P * h : 2 * P * (h + 1)].bitcast(FP4X4),
-                        lhsT_scale=xt_plane[:, z, P * h : P * (h + 1)],
+                        lhsT_scale=planes[:, z, XT_AT + P * h : XT_AT + P * (h + 1)],
                         rhs=picked[z][a][:].bitcast(FP8X4),
-                        rhs_scale=picked_plane[:, z, a * JH : (a + 1) * JH],
-                        start=(z == 0 and h == 0),
-                        stop=(z == PASSES - 1 and h == TILES - 1),
+                        rhs_scale=planes[:, z, a * JH : (a + 1) * JH],
+                        start=(z == 0),
+                        stop=(z == PASSES - 1),
                     )
 
         xs_grouped = keep.tile([P, T, PACK], BF16, name="xs_grouped", align_bytes=64)
@@ -99,46 +99,45 @@ def tile_list_class_families_kernel(tc, xt_words, xt_scales, wc_words, wc_scales
         fam_max = keep.tile([P, TILES, B], F32, name="fam_max")
         shifted = keep.tile([P, HALVES, TILES, JH], F32, name="shifted")
         expd = keep.tile([P, HALVES, TILES, JH], F32, name="expd")
-        for a in range(HALVES):
-            nc.vector.tensor_reduce(
-                out=fam_max[:, :, a * BH : (a + 1) * BH],
-                in_=logits[a][:].rearrange("p h (b s) -> p h b s", s=SLOTS),
-                axis=AXIS.X,
-                op=ALU.max,
-            )
         neg_row_max = keep.tile([P, TILES], F32, name="neg_row_max")
-        nc.vector.tensor_reduce(out=neg_row_max[:], in_=fam_max[:], axis=AXIS.X, op=ALU.max, negate=True)
         weight = keep.tile([P, TILES, B], F32, name="weight")
-        for h in range(TILES):
-            nc.scalar.activation(out=weight[:, h, :], in_=fam_max[:, h, :], func=ACT.Exp, bias=neg_row_max[:, h : h + 1])
-        for a, tiles in ((0, slice(0, 2)), (1, slice(0, 1)), (1, slice(1, 2))):
-            n = tiles.stop - tiles.start
-            nc.vector.tensor_tensor(
-                out=shifted[:, a, tiles, :].rearrange("p h (b s) -> p h b s", s=SLOTS),
-                in0=logits[a][:, tiles, :].rearrange("p h (b s) -> p h b s", s=SLOTS),
-                in1=fam_max[:, tiles, a * BH : (a + 1) * BH].unsqueeze(3).to_broadcast([P, n, BH, SLOTS]),
-                op=ALU.subtract,
-            )
-            nc.scalar.activation(out=expd[:, a, tiles, :], in_=shifted[:, a, tiles, :], func=ACT.Exp)
+        for a in range(HALVES):
+            for h in range(TILES):
+                nc.vector.tensor_reduce(
+                    out=fam_max[:, h, a * BH : (a + 1) * BH],
+                    in_=logits[a][h][:].rearrange("p (b s) -> p b s", s=SLOTS),
+                    axis=AXIS.X,
+                    op=ALU.max,
+                )
+            if a == HALVES - 1:
+                nc.vector.tensor_reduce(out=neg_row_max[:], in_=fam_max[:], axis=AXIS.X, op=ALU.max, negate=True)
+                for h in range(TILES):
+                    nc.scalar.activation(
+                        out=weight[:, h, :], in_=fam_max[:, h, :], func=ACT.Exp, bias=neg_row_max[:, h : h + 1]
+                    )
+            for h in range(TILES):
+                nc.vector.tensor_tensor(
+                    out=shifted[:, a, h, :].rearrange("p (b s) -> p b s", s=SLOTS),
+                    in0=logits[a][h][:].rearrange("p (b s) -> p b s", s=SLOTS),
+                    in1=fam_max[:, h, a * BH : (a + 1) * BH].unsqueeze(2).to_broadcast([P, BH, SLOTS]),
+                    op=ALU.subtract,
+                )
+                nc.scalar.activation(out=expd[:, a, h, :], in_=shifted[:, a, h, :], func=ACT.Exp)
 
-        below = keep.tile([P, TILES, B], F32, name="below")
-        nc.vector.tensor_tensor(
-            out=below[:], in0=fam_max[:], in1=neg_row_max[:].unsqueeze(2).to_broadcast([P, TILES, B]), op=ALU.add
-        )
         xs_codes = keep.tile([P, T], U32, name="xs_codes", align_bytes=64)
         xs_plane = keep.tile([P, T], U8, name="xs_plane", align_bytes=64)
         nc.vector.quantize_mx(
             out=xs_codes[:].bitcast(FP8X4), scales=xs_plane[:], in_=xs_grouped[:].rearrange("p t j -> p (t j)")
         )
         base = keep.tile([P, TILES, B], F32, name="base")
-        fam = [psum.tile([P, B], F32, name=f"fam{h}") for h in range(TILES)]
+        fam = psum.tile([P, TILES, B], F32, name="fam")
         for h in range(TILES):
             nc.tensor.matmul_mx(
-                out=fam[h][:],
+                out=fam[:, h, :],
                 lhsT=xs_codes[:, P * h : P * (h + 1)].bitcast(FP8X4),
                 lhsT_scale=xs_plane[:, P * h : P * (h + 1)],
                 rhs=ws_codes[:].bitcast(FP4X4),
-                rhs_scale=ws_plane[:, 0, :],
+                rhs_scale=planes[:, 0, WS_AT:ROW],
                 start=True,
                 stop=True,
             )
@@ -163,10 +162,17 @@ def tile_list_class_families_kernel(tc, xt_words, xt_scales, wc_words, wc_scales
                 op1=ALU.mult,
                 accum_out=sums[:, h, B : B + 1],
             )
+        below = keep.tile([P, TILES, B], F32, name="below")
         for h in range(TILES):
-            nc.vector.scalar_tensor_tensor(
-                out=base[:, h, :], in0=fam[h][:], scalar=0.5, in1=below[:, h, :], op0=ALU.mult, op1=ALU.add
+            nc.gpsimd.tensor_scalar(
+                out=below[:, h, :],
+                in0=fam_max[:, h, :],
+                scalar1=neg_row_max[:, h : h + 1],
+                scalar2=1.0,
+                op0=ALU.add,
+                op1=ALU.mult,
             )
+        nc.vector.scalar_tensor_tensor(out=base[:], in0=fam[:], scalar=0.5, in1=below[:], op0=ALU.mult, op1=ALU.add)
 
         logs = keep.tile([P, TILES, B + 1], F32, name="logs")
         nc.scalar.activation(out=logs[:], in_=sums[:], func=ACT.Ln)

@@ -47,10 +47,10 @@ def tile_list_class_families_kernel(tc, xt_words, xt_scales, wc_words, wc_scales
         nc.gpsimd.memset(planes[:].bitcast(I32), 0)
 
         table = [keep.tile([P, C], I32, name=f"table{z}", align_bytes=64) for z in range(PASSES)]
-        xs_raw = reuse.tile([P, PACK, T], F32, name="xs_raw", align_bytes=64, offset=0)
-        picked_rows = reuse.tile([P, J], U8, name="picked_rows", align_bytes=64, offset=0)
+        xs_raw = reuse.tile([P, PACK, T], F32, name="xs_raw", align_bytes=64, offset=4096)
+        picked_rows = reuse.tile([P, J], U8, name="picked_rows", align_bytes=64, offset=8192 - 128)
         xt_codes = keep.tile([P, PASSES, 2 * T], U8, name="xt_codes", align_bytes=64)
-        ws_codes = keep.tile([P, 2 * B], U8, name="ws_codes", align_bytes=64)
+        ws_codes = reuse.tile([P, 2 * B], U8, name="ws_codes", align_bytes=64, offset=8192)
 
         nc.sync.dma_start(
             out=wc_rows[ROWS_AT:P, :].bitcast(I32), in_=wc_scales.rearrange("z g c -> g z c").bitcast(I32)
@@ -63,7 +63,6 @@ def tile_list_class_families_kernel(tc, xt_words, xt_scales, wc_words, wc_scales
         nc.sync.dma_start(out=stage[ROWS_AT:P:PASSES, WS_AT:ROW].bitcast(I32), in_=ws_scales[0].bitcast(I32))
         nc.sync.dma_start(out=table[1][:], in_=wc_words[1].rearrange("p c r -> p (c r)").bitcast(I32))
         nc.sync.dma_start(out=xt_codes[:].bitcast(I32), in_=xt_words.rearrange("z p b -> p z b").bitcast(I32))
-        nc.sync.dma_start(out=ws_codes[:].bitcast(I32), in_=ws_words[0].bitcast(I32))
 
         nc.vector.tensor_copy(picked_rows[:], wc_rows[:].indirect(offsets[:]))
         nc.vector.tensor_copy(stage[ROWS_AT:P, 0:J].bitcast(I32), picked_rows[ROWS_AT:P, :].bitcast(I32))
@@ -73,8 +72,18 @@ def tile_list_class_families_kernel(tc, xt_words, xt_scales, wc_words, wc_scales
                 in_=stage[ROWS_AT + 8 * q : ROWS_AT + 8 * q + 8, :].bitcast(I32),
             )
         nc.sync.dma_start(out=xs_raw[:], in_=xs.rearrange("(p j) t -> p j t", j=PACK))
+        nc.sync.dma_start(out=ws_codes[:].bitcast(I32), in_=ws_words[0].bitcast(I32))
 
-        picked = [[keep.tile([P, JH], U32, name=f"picked{z}{a}", align_bytes=64) for a in range(HALVES)] for z in range(PASSES)]
+        picked = [
+            [
+                keep.tile([P, JH], U32, name="picked00", align_bytes=64),
+                reuse.tile([P, JH], U32, name="picked01", align_bytes=64, offset=1024),
+            ],
+            [
+                keep.tile([P, JH], U32, name="picked10", align_bytes=64),
+                reuse.tile([P, JH], U32, name="picked11", align_bytes=64, offset=2048),
+            ],
+        ]
         logits = [[psum.tile([P, JH], F32, name=f"logits{a}{h}") for h in range(TILES)] for a in range(HALVES)]
         for z in range(PASSES):
             for a in range(HALVES):
@@ -94,37 +103,52 @@ def tile_list_class_families_kernel(tc, xt_words, xt_scales, wc_words, wc_scales
                     )
 
         xs_grouped = keep.tile([P, T, PACK], BF16, name="xs_grouped", align_bytes=64)
-        nc.scalar.copy(out=xs_grouped[:], in_=xs_raw[:].rearrange("p j t -> p t j"))
+        nc.gpsimd.tensor_scalar(
+            out=xs_grouped[:], in0=xs_raw[:].rearrange("p j t -> p t j"), scalar1=1.0, scalar2=0.0, op0=ALU.mult, op1=ALU.add
+        )
 
         fam_max = keep.tile([P, TILES, B], F32, name="fam_max")
-        shifted = keep.tile([P, HALVES, TILES, JH], F32, name="shifted")
+        shifted = [
+            [
+                reuse.tile([P, JH], F32, name=f"shifted{a}{h}", align_bytes=64, offset=1024 * (TILES * a + h))
+                for h in range(TILES)
+            ]
+            for a in range(HALVES)
+        ]
         expd = keep.tile([P, HALVES, TILES, JH], F32, name="expd")
         neg_row_max = keep.tile([P, TILES], F32, name="neg_row_max")
         weight = keep.tile([P, TILES, B], F32, name="weight")
-        for a in range(HALVES):
-            for h in range(TILES):
-                nc.vector.tensor_reduce(
-                    out=fam_max[:, h, a * BH : (a + 1) * BH],
-                    in_=logits[a][h][:].rearrange("p (b s) -> p b s", s=SLOTS),
-                    axis=AXIS.X,
-                    op=ALU.max,
-                )
-            if a == HALVES - 1:
-                nc.vector.tensor_reduce(out=neg_row_max[:], in_=fam_max[:], axis=AXIS.X, op=ALU.max, negate=True)
-                for h in range(TILES):
-                    nc.scalar.activation(
-                        out=weight[:, h, :], in_=fam_max[:, h, :], func=ACT.Exp, bias=neg_row_max[:, h : h + 1]
-                    )
-            for h in range(TILES):
-                nc.vector.tensor_tensor(
-                    out=shifted[:, a, h, :].rearrange("p (b s) -> p b s", s=SLOTS),
-                    in0=logits[a][h][:].rearrange("p (b s) -> p b s", s=SLOTS),
-                    in1=fam_max[:, h, a * BH : (a + 1) * BH].unsqueeze(2).to_broadcast([P, BH, SLOTS]),
-                    op=ALU.subtract,
-                )
-                nc.scalar.activation(out=expd[:, a, h, :], in_=shifted[:, a, h, :], func=ACT.Exp)
+        pieces = [(a, h) for a in range(HALVES) for h in range(TILES)]
 
-        xs_codes = keep.tile([P, T], U32, name="xs_codes", align_bytes=64)
+        def take_max(a, h):
+            nc.vector.tensor_reduce(
+                out=fam_max[:, h, a * BH : (a + 1) * BH],
+                in_=logits[a][h][:].rearrange("p (b s) -> p b s", s=SLOTS),
+                axis=AXIS.X,
+                op=ALU.max,
+            )
+
+        def shift_and_exp(a, h):
+            nc.vector.tensor_tensor(
+                out=shifted[a][h][:].rearrange("p (b s) -> p b s", s=SLOTS),
+                in0=logits[a][h][:].rearrange("p (b s) -> p b s", s=SLOTS),
+                in1=fam_max[:, h, a * BH : (a + 1) * BH].unsqueeze(2).to_broadcast([P, BH, SLOTS]),
+                op=ALU.subtract,
+            )
+            nc.scalar.activation(out=expd[:, a, h, :], in_=shifted[a][h][:], func=ACT.Exp)
+
+        take_max(*pieces[0])
+        shift_and_exp(*pieces[0])
+        take_max(*pieces[1])
+        for before, piece in zip(pieces[1:], pieces[2:]):
+            take_max(*piece)
+            shift_and_exp(*before)
+        nc.vector.tensor_reduce(out=neg_row_max[:], in_=fam_max[:], axis=AXIS.X, op=ALU.max, negate=True)
+        for h in range(TILES):
+            nc.scalar.activation(out=weight[:, h, :], in_=fam_max[:, h, :], func=ACT.Exp, bias=neg_row_max[:, h : h + 1])
+        shift_and_exp(*pieces[-1])
+
+        xs_codes = reuse.tile([P, T], U32, name="xs_codes", align_bytes=64, offset=2048)
         xs_plane = keep.tile([P, T], U8, name="xs_plane", align_bytes=64)
         nc.vector.quantize_mx(
             out=xs_codes[:].bitcast(FP8X4), scales=xs_plane[:], in_=xs_grouped[:].rearrange("p t j -> p (t j)")
@@ -175,9 +199,9 @@ def tile_list_class_families_kernel(tc, xt_words, xt_scales, wc_words, wc_scales
         nc.vector.scalar_tensor_tensor(out=base[:], in0=fam[:], scalar=0.5, in1=below[:], op0=ALU.mult, op1=ALU.add)
 
         logs = keep.tile([P, TILES, B + 1], F32, name="logs")
-        nc.scalar.activation(out=logs[:], in_=sums[:], func=ACT.Ln)
         result = keep.tile([P, TILES, B], F32, name="result")
         for h in range(TILES):
+            nc.scalar.activation(out=logs[:, h, :], in_=sums[:, h, :], func=ACT.Ln)
             nc.vector.scalar_tensor_tensor(
                 out=result[:, h, :],
                 in0=logs[:, h, 0:B],
@@ -186,4 +210,4 @@ def tile_list_class_families_kernel(tc, xt_words, xt_scales, wc_words, wc_scales
                 op0=ALU.subtract,
                 op1=ALU.add,
             )
-        nc.sync.dma_start(out=out.rearrange("(h p) b -> p h b", p=P), in_=result[:])
+            nc.sync.dma_start(out=out[P * h : P * (h + 1), :], in_=result[:, h, :])

from contextlib import ExitStack

import concourse.mybir as mybir

K, T, C, J, B, L = 1024, 256, 2048, 512, 64, 512
FLOPS = 2 * T * K * J + 2 * T * L * B

F32 = mybir.dt.float32
BF16 = mybir.dt.bfloat16
I32 = mybir.dt.int32
U32 = mybir.dt.uint32
U16 = mybir.dt.uint16
U8 = mybir.dt.uint8
FP8X4 = mybir.dt.float8_e4m3fn_x4
FP4X4 = mybir.dt.float4_e2m1fn_x4
ALU = mybir.AluOpType
ACT = mybir.ActivationFunctionType
AXIS = mybir.AxisListType

P = 128
PACK = 4
PASSES = K // (P * PACK)
TILES = T // P
SLOTS = J // B
HALVES = 2
JH = J // HALVES
BH = B // HALVES
ROWS_AT = P - 16 * PASSES
XT_AT = J
WS_AT = XT_AT + T
ROW = WS_AT + B


def tile_list_class_families_kernel(tc, xt_words, xt_scales, wc_words, wc_scales, xs, ws_words, ws_scales, offs, out):
    nc = tc.nc
    with ExitStack() as ctx:
        keep = ctx.enter_context(tc.tile_pool(name="keep", bufs=1))
        psum = ctx.enter_context(tc.psum_pool(name="psum", bufs=1))

        reuse = ctx.enter_context(tc.tile_pool(name="reuse", bufs=1))
        offsets = keep.tile([P, J // 16], U16, name="offsets")
        wc_rows = keep.tile([P, C], U8, name="wc_rows", align_bytes=64)
        stage = keep.tile([P, ROW], U8, name="stage", align_bytes=64)
        planes = keep.tile([P, PASSES, ROW], U8, name="planes", align_bytes=64)
        nc.gpsimd.memset(stage[ROWS_AT:P, WS_AT:ROW].bitcast(I32), 0)
        nc.vector.memset(wc_rows[0:ROWS_AT, :].bitcast(I32), 0)
        nc.gpsimd.memset(planes[:].bitcast(I32), 0)

        table = [keep.tile([P, C], I32, name=f"table{z}", align_bytes=64) for z in range(PASSES)]
        xs_raw = reuse.tile([P, PACK, T], F32, name="xs_raw", align_bytes=64, offset=4096)
        picked_rows = reuse.tile([P, J], U8, name="picked_rows", align_bytes=64, offset=8192 - 128)
        xt_codes = keep.tile([P, PASSES, 2 * T], U8, name="xt_codes", align_bytes=64)
        ws_codes = reuse.tile([P, 2 * B], U8, name="ws_codes", align_bytes=64, offset=8192)

        nc.sync.dma_start(
            out=wc_rows[ROWS_AT:P, :].bitcast(I32), in_=wc_scales.rearrange("z g c -> g z c").bitcast(I32)
        )
        nc.sync.dma_start(offsets[:], offs)
        nc.sync.dma_start(out=table[0][:], in_=wc_words[0].rearrange("p c r -> p (c r)").bitcast(I32))
        nc.sync.dma_start(
            out=stage[ROWS_AT:P, XT_AT:WS_AT].bitcast(I32), in_=xt_scales.rearrange("z g c -> g z c").bitcast(I32)
        )
        nc.sync.dma_start(out=stage[ROWS_AT:P:PASSES, WS_AT:ROW].bitcast(I32), in_=ws_scales[0].bitcast(I32))
        nc.sync.dma_start(out=table[1][:], in_=wc_words[1].rearrange("p c r -> p (c r)").bitcast(I32))
        nc.sync.dma_start(out=xt_codes[:].bitcast(I32), in_=xt_words.rearrange("z p b -> p z b").bitcast(I32))

        nc.vector.tensor_copy(picked_rows[:], wc_rows[:].indirect(offsets[:]))
        nc.vector.tensor_copy(stage[ROWS_AT:P, 0:J].bitcast(I32), picked_rows[ROWS_AT:P, :].bitcast(I32))
        for q in range(4):
            nc.sync.dma_start(
                out=planes[32 * q : 32 * q + 4, :, :].bitcast(I32),
                in_=stage[ROWS_AT + 8 * q : ROWS_AT + 8 * q + 8, :].bitcast(I32),
            )
        nc.sync.dma_start(out=xs_raw[:], in_=xs.rearrange("(p j) t -> p j t", j=PACK))
        nc.sync.dma_start(out=ws_codes[:].bitcast(I32), in_=ws_words[0].bitcast(I32))

        picked = [
            [
                keep.tile([P, JH], U32, name="picked00", align_bytes=64),
                reuse.tile([P, JH], U32, name="picked01", align_bytes=64, offset=1024),
            ],
            [
                keep.tile([P, JH], U32, name="picked10", align_bytes=64),
                reuse.tile([P, JH], U32, name="picked11", align_bytes=64, offset=2048),
            ],
        ]
        logits = [[psum.tile([P, JH], F32, name=f"logits{a}{h}") for h in range(TILES)] for a in range(HALVES)]
        for z in range(PASSES):
            for a in range(HALVES):
                cols = slice(a * JH // 16, (a + 1) * JH // 16)
                nc.vector.tensor_copy(picked[z][a][:], table[z][:].bitcast(U32).indirect(offsets[:, cols]))
        for a in range(HALVES):
            for h in range(TILES):
                for z in range(PASSES):
                    nc.tensor.matmul_mx(
                        out=logits[a][h][:],
                        lhsT=xt_codes[:, z, 2 * P * h : 2 * P * (h + 1)].bitcast(FP4X4),
                        lhsT_scale=planes[:, z, XT_AT + P * h : XT_AT + P * (h + 1)],
                        rhs=picked[z][a][:].bitcast(FP8X4),
                        rhs_scale=planes[:, z, a * JH : (a + 1) * JH],
                        start=(z == 0),
                        stop=(z == PASSES - 1),
                    )

        xs_grouped = keep.tile([P, T, PACK], BF16, name="xs_grouped", align_bytes=64)
        nc.gpsimd.tensor_scalar(
            out=xs_grouped[:], in0=xs_raw[:].rearrange("p j t -> p t j"), scalar1=1.0, scalar2=0.0, op0=ALU.mult, op1=ALU.add
        )

        fam_max = keep.tile([P, TILES, B], F32, name="fam_max")
        shifted = [
            [
                reuse.tile([P, JH], F32, name=f"shifted{a}{h}", align_bytes=64, offset=1024 * (TILES * a + h))
                for h in range(TILES)
            ]
            for a in range(HALVES)
        ]
        expd = keep.tile([P, HALVES, TILES, JH], F32, name="expd")
        neg_row_max = keep.tile([P, TILES], F32, name="neg_row_max")
        weight = keep.tile([P, TILES, B], F32, name="weight")
        pieces = [(a, h) for a in range(HALVES) for h in range(TILES)]

        def take_max(a, h):
            nc.vector.tensor_reduce(
                out=fam_max[:, h, a * BH : (a + 1) * BH],
                in_=logits[a][h][:].rearrange("p (b s) -> p b s", s=SLOTS),
                axis=AXIS.X,
                op=ALU.max,
            )

        def shift_and_exp(a, h):
            nc.vector.tensor_tensor(
                out=shifted[a][h][:].rearrange("p (b s) -> p b s", s=SLOTS),
                in0=logits[a][h][:].rearrange("p (b s) -> p b s", s=SLOTS),
                in1=fam_max[:, h, a * BH : (a + 1) * BH].unsqueeze(2).to_broadcast([P, BH, SLOTS]),
                op=ALU.subtract,
            )
            nc.scalar.activation(out=expd[:, a, h, :], in_=shifted[a][h][:], func=ACT.Exp)

        take_max(*pieces[0])
        shift_and_exp(*pieces[0])
        take_max(*pieces[1])
        for before, piece in zip(pieces[1:], pieces[2:]):
            take_max(*piece)
            shift_and_exp(*before)
        nc.vector.tensor_reduce(out=neg_row_max[:], in_=fam_max[:], axis=AXIS.X, op=ALU.max, negate=True)
        for h in range(TILES):
            nc.scalar.activation(out=weight[:, h, :], in_=fam_max[:, h, :], func=ACT.Exp, bias=neg_row_max[:, h : h + 1])
        shift_and_exp(*pieces[-1])

        xs_codes = reuse.tile([P, T], U32, name="xs_codes", align_bytes=64, offset=2048)
        xs_plane = keep.tile([P, T], U8, name="xs_plane", align_bytes=64)
        nc.vector.quantize_mx(
            out=xs_codes[:].bitcast(FP8X4), scales=xs_plane[:], in_=xs_grouped[:].rearrange("p t j -> p (t j)")
        )
        base = keep.tile([P, TILES, B], F32, name="base")
        fam = psum.tile([P, TILES, B], F32, name="fam")
        for h in range(TILES):
            nc.tensor.matmul_mx(
                out=fam[:, h, :],
                lhsT=xs_codes[:, P * h : P * (h + 1)].bitcast(FP8X4),
                lhsT_scale=xs_plane[:, P * h : P * (h + 1)],
                rhs=ws_codes[:].bitcast(FP4X4),
                rhs_scale=planes[:, 0, WS_AT:ROW],
                start=True,
                stop=True,
            )

        sums = keep.tile([P, TILES, B + 1], F32, name="sums")
        for a in range(HALVES):
            nc.vector.tensor_reduce(
                out=sums[:, :, a * BH : (a + 1) * BH],
                in_=expd[:, a, :, :].rearrange("p h (b s) -> p h b s", s=SLOTS),
                axis=AXIS.X,
                op=ALU.add,
            )

        weighted = keep.tile([P, TILES, B], F32, name="weighted")
        for h in range(TILES):
            nc.vector.scalar_tensor_tensor(
                out=weighted[:, h, :],
                in0=sums[:, h, 0:B],
                scalar=1.0,
                in1=weight[:, h, :],
                op0=ALU.mult,
                op1=ALU.mult,
                accum_out=sums[:, h, B : B + 1],
            )
        below = keep.tile([P, TILES, B], F32, name="below")
        for h in range(TILES):
            nc.gpsimd.tensor_scalar(
                out=below[:, h, :],
                in0=fam_max[:, h, :],
                scalar1=neg_row_max[:, h : h + 1],
                scalar2=1.0,
                op0=ALU.add,
                op1=ALU.mult,
            )
        nc.vector.scalar_tensor_tensor(out=base[:], in0=fam[:], scalar=0.5, in1=below[:], op0=ALU.mult, op1=ALU.add)

        logs = keep.tile([P, TILES, B + 1], F32, name="logs")
        result = keep.tile([P, TILES, B], F32, name="result")
        for h in range(TILES):
            nc.scalar.activation(out=logs[:, h, :], in_=sums[:, h, :], func=ACT.Ln)
            nc.vector.scalar_tensor_tensor(
                out=result[:, h, :],
                in0=logs[:, h, 0:B],
                scalar=logs[:, h, B : B + 1],
                in1=base[:, h, :],
                op0=ALU.subtract,
                op1=ALU.add,
            )
            nc.sync.dma_start(out=out[P * h : P * (h + 1), :], in_=result[:, h, :])
